import numpy as np
import ml_dtypes


def mxq(x, axis, fmt="e4m3"):
    dtype, down = {"e4m3": (ml_dtypes.float8_e4m3fn, 7), "e5m2": (ml_dtypes.float8_e5m2, 14)}[fmt]
    v = np.moveaxis(np.asarray(x, np.float32).astype(ml_dtypes.bfloat16).astype(np.float64), axis, -1)
    blocks = v.reshape(v.shape[:-1] + (-1, 32))
    amax = np.abs(blocks).max(-1, keepdims=True)
    byte = np.maximum(np.where(amax > 0, np.frexp(amax)[1] - 1 + 127, 0) - down, 1)
    scale = np.exp2(byte - 127.0)
    codes = (blocks / scale).astype(np.float32).astype(dtype).astype(np.float64)
    return np.moveaxis((codes * scale).reshape(v.shape), -1, axis)


WIDE = False


def mx_kscale(k):
    if not WIDE:
        return np.ones(k)
    levels = np.array([30, -30])
    if k % 512:
        return np.exp2(np.random.permutation(np.resize(levels, k // 32))).repeat(32)
    a = np.empty((k // 512, 16))
    for p in range(k // 512):
        a[p, :8] = np.random.permutation(np.resize(levels, 8))
        for g in range(8):
            far = levels[np.abs(levels - a[p, g]) >= 10]
            a[p, g + 8] = far[np.random.randint(len(far))]
    return np.exp2(a.ravel()).repeat(32)


def f64(x):
    return np.asarray(x).astype(np.float64)


def striped(idx):
    return np.tile(np.asarray(idx).reshape(-1, 16).T, (8, 1)).astype(np.uint16)


def unstriped(offs):
    return offs[:16].T.reshape(-1).astype(np.int64)


E2M1 = np.array([0.0, 0.5, 1.0, 1.5, 2.0, 3.0, 4.0, 6.0, -0.0, -0.5, -1.0, -1.5, -2.0, -3.0, -4.0, -6.0])


def pack_weight(w, fmt):
    k, n = w.shape
    w = f64(np.asarray(w, np.float32).astype(ml_dtypes.bfloat16)).reshape(k // 32, 32, n)
    amax = np.abs(w).max(1)
    if fmt == "e4m3":
        byte = np.frexp(amax)[1] - 1 + 127 - 7
    else:
        mant, ex = np.frexp(amax / 6.0)
        byte = np.where(mant > 0.5, ex, ex - 1) + 127
    byte = np.clip(np.where(amax > 0, byte, 1), 1, 254)
    scaled = (w * np.exp2(127.0 - byte)[:, None, :]).reshape(k, n).astype(np.float32)
    by_word = np.ascontiguousarray(scaled.reshape(k // 512, 128, 4, n).transpose(0, 1, 3, 2))
    if fmt == "e4m3":
        words = by_word.astype(ml_dtypes.float8_e4m3fn).view(np.uint8)
    else:
        c = by_word.astype(ml_dtypes.float4_e2m1fn).view(np.uint8) & 0xF
        words = (c[..., 0::2] | (c[..., 1::2] << 4)).reshape(k // 512, 128, 2 * n)
    return np.ascontiguousarray(words), np.ascontiguousarray(byte.astype(np.uint8).reshape(k // 512, 16, n))


def unpack_weight(words, scales, fmt):
    g, _, n = scales.shape
    words = np.ascontiguousarray(words).reshape(g, 128, n, -1)
    if fmt == "e4m3":
        vals = words.view(ml_dtypes.float8_e4m3fn).astype(np.float64)
    else:
        nib = np.empty((g, 128, n, 4), np.uint8)
        nib[..., 0::2] = words & 0xF
        nib[..., 1::2] = words >> 4
        vals = E2M1[nib]
    vals = vals * np.repeat(np.exp2(scales.astype(np.float64) - 127.0), 8, axis=1)[..., None]
    return vals.transpose(0, 1, 3, 2).reshape(g * 512, n)


K, F, T, Z, J, R, C, O, N, E = 512, 512, 1024, 1024, 256, 512, 512, 256, 256, 1024


def setup_inputs():
    n = np.random.standard_normal
    idx = np.random.permutation(T)[:J]
    idx2 = np.random.permutation(Z)[:J]
    idx3 = np.random.permutation(C)[:J]
    idx4 = np.random.permutation(C)[:J]
    idx5 = np.random.permutation(C)[:O]
    idx6 = np.random.permutation(C)[:O]
    idx7 = np.random.permutation(E)[:O]
    fk = mx_kscale(K)
    fr = mx_kscale(R)
    ff = mx_kscale(F)
    xtp = pack_weight(n((K, T)) / fk[:, None], "e2m1")
    wp = pack_weight(n((K, R)) * 1 / np.sqrt(K) * fk[:, None] * fr, "e4m3")
    xop = pack_weight(n((F, Z)) / ff[:, None], "e4m3")
    w2p = pack_weight(n((F, R)) * 1 / np.sqrt(F) * ff[:, None] * fr, "e2m1")
    wbp = pack_weight(n((R, N)) * 1 / np.sqrt(R) / fr[:, None], "e2m1")
    return {
        "xt_words": xtp[0],
        "xt_scales": xtp[1],
        "w_words": wp[0],
        "w_scales": wp[1],
        "xo_words": xop[0],
        "xo_scales": xop[1],
        "w2_words": w2p[0],
        "w2_scales": w2p[1],
        "wb_words": wbp[0],
        "wb_scales": wbp[1],
        "tz": (n((N, E))).astype(np.float32),
        "offs": striped(idx),
        "offs2": striped(idx2),
        "offs3": striped(idx3),
        "offs4": striped(idx4),
        "offs5": striped(idx5),
        "offs6": striped(idx6),
        "offs7": striped(idx7),
    }


def reference(xt_words, xt_scales, w_words, w_scales, xo_words, xo_scales, w2_words, w2_scales, wb_words, wb_scales, tz, offs, offs2, offs3, offs4, offs5, offs6, offs7):
    idx = unstriped(offs)
    idx2 = unstriped(offs2)
    idx3 = unstriped(offs3)
    idx4 = unstriped(offs4)
    idx5 = unstriped(offs5)
    idx6 = unstriped(offs6)
    idx7 = unstriped(offs7)
    xtu = unpack_weight(xt_words, xt_scales, "e2m1")
    wu = unpack_weight(w_words, w_scales, "e4m3")
    xou = unpack_weight(xo_words, xo_scales, "e4m3")
    w2u = unpack_weight(w2_words, w2_scales, "e2m1")
    wbu = unpack_weight(wb_words, wb_scales, "e2m1")
    xtidxg = xtu[:, idx]
    a = wu.T @ xtidxg
    xoidx2g = xou[:, idx2]
    b = w2u.T @ xoidx2g
    pw = np.zeros((R, C))
    pw[:, idx3] = a
    pv = np.zeros((R, C))
    pv[:, idx4] = b
    hid = np.maximum(pw[:, idx5], pv[:, idx6])
    hidq = mxq(hid, 0, "e5m2")
    p = wbu.T @ hidq
    y = p + f64(tz)[:, idx7]
    return y

@@ -1,0 +1,175 @@
+from contextlib import ExitStack
+
+import concourse.mybir as mybir
+
+F32 = mybir.dt.float32
+BF16 = mybir.dt.bfloat16
+I32 = mybir.dt.int32
+U32 = mybir.dt.uint32
+U16 = mybir.dt.uint16
+U8 = mybir.dt.uint8
+E4M3X4 = mybir.dt.float8_e4m3fn_x4
+E5M2X4 = mybir.dt.float8_e5m2_x4
+E2M1X4 = mybir.dt.float4_e2m1fn_x4
+COPY = mybir.ActivationFunctionType.Copy
+MAX = mybir.AluOpType.max
+ADD = mybir.AluOpType.add
+
+P = 128
+PACK = 4
+T, Z, J, R, C, O, N, E = 1024, 1024, 256, 512, 512, 256, 256, 1024
+HALVES = 2
+OH = O // HALVES
+FLOPS = 2 * 512 * R * J * 2 + 2 * R * N * O
+
+
+def tile_list_twotab_twoboards_one_tabled_kernel(
+    tc, xt_words, xt_scales, w_words, w_scales, xo_words, xo_scales, w2_words, w2_scales,
+    wb_words, wb_scales, tz, offs, offs2, offs3, offs4, offs5, offs6, offs7, out,
+):
+    nc = tc.nc
+    with ExitStack() as ctx:
+        keep = ctx.enter_context(tc.tile_pool(name="keep", bufs=1))
+        psum = ctx.enter_context(tc.psum_pool(name="psum", bufs=8))
+
+        def load_list(src, name):
+            tile = keep.tile([P, src.shape[1]], U16, name=name)
+            nc.sync.dma_start(tile[:], src)
+            return tile
+
+        def load_words(queue, src, dtype, cols, name):
+            tile = keep.tile([P, cols], dtype, name=name, align_bytes=64)
+            queue.dma_start(tile[:].bitcast(I32), src.bitcast(I32))
+            return tile
+
+        def load_scales(queue, src, cols, name):
+            tile = keep.tile([P, cols], U8, name=name, align_bytes=64)
+            rows = src[0].bitcast(I32)
+            for q in range(4):
+                queue.dma_start(
+                    tile[32 * q:32 * (q + 1), :].bitcast(I32),
+                    rows[4 * q:4 * (q + 1), :].unsqueeze(0).to_broadcast([8, 4, cols // 4]),
+                )
+            return tile
+
+        l_xt = load_list(offs, "l_xt")
+        xt_s = load_scales(nc.scalar, xt_scales, T, "xt_s")
+        xt_w = load_words(nc.sync, xt_words[0], U16, T, "xt_w")
+        w_w = load_words(nc.sync, w_words[0].rearrange("p n t -> p (n t)"), U32, R, "w_w")
+        w_s = load_scales(nc.sync, w_scales, R, "w_s")
+        l_xo = load_list(offs2, "l_xo")
+        xo_w = load_words(nc.sync, xo_words[0].rearrange("p n t -> p (n t)"), U32, Z, "xo_w")
+        w2_w = load_words(nc.sync, w2_words[0], U16, R, "w2_w")
+        l_put = [load_list(offs3, "l_put_a")]
+        xo_s = load_scales(nc.sync, xo_scales, Z, "xo_s")
+        w2_s = load_scales(nc.sync, w2_scales, R, "w2_s")
+        l_put.append(load_list(offs4, "l_put_b"))
+        l_get = [load_list(offs5, "l_get_a"), load_list(offs6, "l_get_b")]
+        l_tz = load_list(offs7, "l_tz")
+        tz_sb = []
+        for nt in range(N // P):
+            tile = keep.tile([P, E], F32, name=f"tz{nt}")
+            nc.sync.dma_start(tile[:], tz[nt * P:(nt + 1) * P, :])
+            tz_sb.append(tile)
+        wb_w = load_words(nc.sync, wb_words[0], U16, N, "wb_w")
+        wb_s = load_scales(nc.sync, wb_scales, N, "wb_s")
+
+        boards = [[keep.tile([P, C], F32, name=f"board{b}_{t}") for t in range(PACK)] for b in range(2)]
+        for b in range(2):
+            for t in range(PACK):
+                (nc.vector, nc.gpsimd)[b].memset(boards[b][t][:], 0.0)
+
+        def gather_bytes(window, lst, dtype, name):
+            tile = keep.tile([P, J], dtype, name=name, align_bytes=64)
+            nc.vector.tensor_copy(tile[:], window[:].indirect(lst[:]))
+            return tile
+
+        def deal(src, dtype, view, name):
+            tile = keep.tile([P, R], dtype, name=name, align_bytes=64)
+            nc.vector.tensor_copy(
+                tile[:].bitcast(view).rearrange("p (t m) -> p m t", t=PACK),
+                src[:].bitcast(view).rearrange("p (m t) -> p m t", t=PACK),
+            )
+            return tile
+
+        xt_gw = gather_bytes(xt_w, l_xt, U16, "xt_gw")
+        w_dw = deal(w_w, U32, I32, "w_dw")
+        xt_gs = gather_bytes(xt_s, l_xt, U8, "xt_gs")
+        w_ds = deal(w_s, U8, U8, "w_ds")
+        xo_gw = gather_bytes(xo_w, l_xo, U32, "xo_gw")
+        w2_dw = deal(w2_w, U16, U16, "w2_dw")
+        xo_gs = gather_bytes(xo_s, l_xo, U8, "xo_gs")
+        w2_ds = deal(w2_s, U8, U8, "w2_ds")
+
+        stationary = [(w_dw, w_ds, E4M3X4), (w2_dw, w2_ds, E2M1X4)]
+        moving = [(xt_gw, xt_gs, E2M1X4), (xo_gw, xo_gs, E4M3X4)]
+
+        def move(on_scalar, dst, src):
+            if on_scalar:
+                nc.scalar.activation(dst, src, COPY)
+            else:
+                nc.vector.tensor_copy(dst, src)
+
+        got_a = keep.tile([P, PACK, O], F32, name="got_a")
+        got_b = [keep.tile([P, PACK, OH], F32, name=f"got_b{h}") for h in range(HALVES)]
+
+        for b in range(2):
+            sw, ss, sfmt = stationary[b]
+            mw, ms, mfmt = moving[b]
+            staged = []
+            for t in range(PACK):
+                cols = slice(t * P, (t + 1) * P)
+                acc = psum.tile([P, J], F32, name="acc")
+                nc.tensor.matmul_mx(
+                    out=acc[:], lhsT=sw[:, cols].bitcast(sfmt), lhsT_scale=ss[:, cols],
+                    rhs=mw[:].bitcast(mfmt), rhs_scale=ms[:], start=True, stop=True,
+                )
+                if (b, t) == (1, 2):
+                    wide = keep.tile([P, N // P, J], F32, name="stage_last", tag="late")
+                    stage = wide[:, 0, :]
+                else:
+                    stage = keep.tile([P, J], F32, name=f"stage{b}_{t}")[:]
+                staged.append((acc, stage))
+            for pair in range(2):
+                for t in (2 * pair, 2 * pair + 1):
+                    nc.scalar.copy(staged[t][1], staged[t][0][:])
+                for t in (2 * pair, 2 * pair + 1):
+                    move(t % 2 == 0, boards[b][t][:].indirect(l_put[b][:]), staged[t][1])
+            if b == 0:
+                for t in range(PACK):
+                    move(t == 0, got_a[:, t, :], boards[0][t][:].indirect(l_get[0][:]))
+
+        cols_h = OH // 16
+        for h in range(HALVES):
+            for t in range(PACK):
+                move(t % 2 == 0, got_b[h][:, t, :], boards[1][t][:].indirect(l_get[1][:, h * cols_h:(h + 1) * cols_h]))
+
+        tz_g = keep.tile([P, N // P, O], F32, name="tz_g", tag="late")
+        for nt in range(N // P):
+            move(True, tz_g[:, nt, :], tz_sb[nt][:].indirect(l_tz[:]))
+
+        hid, codes, plane = [], [], []
+        for h in range(HALVES):
+            hid.append(keep.tile([P, OH, PACK], BF16, name=f"hid{h}", align_bytes=64))
+            nc.vector.tensor_tensor(
+                hid[h][:].rearrange("p (c i) t -> p c t i", i=4),
+                got_a[:, :, h * OH:(h + 1) * OH].rearrange("p t (c i) -> p c t i", i=4),
+                got_b[h][:].rearrange("p t (c i) -> p c t i", i=4),
+                MAX,
+            )
+        for h in range(HALVES):
+            codes.append(keep.tile([P, OH], U32, name=f"codes{h}", align_bytes=64))
+            plane.append(keep.tile([P, OH], U8, name=f"plane{h}", align_bytes=64))
+            nc.vector.quantize_mx(codes[h][:].bitcast(E5M2X4), plane[h][:], hid[h][:].rearrange("p o t -> p (o t)"))
+        out_v = out.rearrange("(nt p) o -> p nt o", p=P)
+        for h in range(HALVES):
+            acc = psum.tile([P, N // P, OH], F32, name="acc")
+            for nt in range(N // P):
+                cols = slice(nt * P, (nt + 1) * P)
+                nc.tensor.matmul_mx(
+                    out=acc[:, nt, :], lhsT=wb_w[:, cols].bitcast(E2M1X4), lhsT_scale=wb_s[:, cols],
+                    rhs=codes[h][:].bitcast(E5M2X4), rhs_scale=plane[h][:], start=True, stop=True,
+                )
+            res = keep.tile([P, N // P, OH], F32, name=f"res{h}")
+            nc.vector.tensor_tensor(res[:], acc[:], tz_g[:, :, h * OH:(h + 1) * OH], ADD)
+            nc.sync.dma_start(out_v[:, :, h * OH:(h + 1) * OH], res[:])

@@ -53,18 +53,19 @@ def tile_list_twotab_twoboards_one_tabled_kernel(
             return tile
 
         l_xt = load_list(offs, "l_xt")
-        xt_s = load_scales(nc.scalar, xt_scales, T, "xt_s")
+        xt_s = load_scales(nc.sync, xt_scales, T, "xt_s")
         xt_w = load_words(nc.sync, xt_words[0], U16, T, "xt_w")
         w_w = load_words(nc.sync, w_words[0].rearrange("p n t -> p (n t)"), U32, R, "w_w")
-        w_s = load_scales(nc.sync, w_scales, R, "w_s")
+        w2_w = load_words(nc.gpsimd, w2_words[0], U16, R, "w2_w")
         l_xo = load_list(offs2, "l_xo")
+        w_s = load_scales(nc.sync, w_scales, R, "w_s")
         xo_w = load_words(nc.sync, xo_words[0].rearrange("p n t -> p (n t)"), U32, Z, "xo_w")
-        w2_w = load_words(nc.sync, w2_words[0], U16, R, "w2_w")
         l_put = [load_list(offs3, "l_put_a")]
         xo_s = load_scales(nc.sync, xo_scales, Z, "xo_s")
         w2_s = load_scales(nc.sync, w2_scales, R, "w2_s")
+        l_get = [load_list(offs5, "l_get_a")]
         l_put.append(load_list(offs4, "l_put_b"))
-        l_get = [load_list(offs5, "l_get_a"), load_list(offs6, "l_get_b")]
+        l_get.append(load_list(offs6, "l_get_b"))
         l_tz = load_list(offs7, "l_tz")
         tz_sb = []
         for nt in range(N // P):
@@ -77,31 +78,36 @@ def tile_list_twotab_twoboards_one_tabled_kernel(
         boards = [[keep.tile([P, C], F32, name=f"board{b}_{t}") for t in range(PACK)] for b in range(2)]
         for b in range(2):
             for t in range(PACK):
-                (nc.vector, nc.gpsimd)[b].memset(boards[b][t][:], 0.0)
+                nc.gpsimd.memset(boards[b][t][:], 0.0)
 
         def gather_bytes(window, lst, dtype, name):
             tile = keep.tile([P, J], dtype, name=name, align_bytes=64)
             nc.vector.tensor_copy(tile[:], window[:].indirect(lst[:]))
             return tile
 
-        def deal(src, dtype, view, name):
+        def deal(copy, src, dtype, name):
             tile = keep.tile([P, R], dtype, name=name, align_bytes=64)
-            nc.vector.tensor_copy(
-                tile[:].bitcast(view).rearrange("p (t m) -> p m t", t=PACK),
-                src[:].bitcast(view).rearrange("p (m t) -> p m t", t=PACK),
+            copy(
+                tile[:].rearrange("p (t m) -> p m t", t=PACK),
+                src[:].rearrange("p (m t) -> p m t", t=PACK),
             )
             return tile
 
         xt_gw = gather_bytes(xt_w, l_xt, U16, "xt_gw")
-        w_dw = deal(w_w, U32, I32, "w_dw")
+        w_dw = deal(nc.scalar.copy, w_w, U32, "w_dw")
         xt_gs = gather_bytes(xt_s, l_xt, U8, "xt_gs")
-        w_ds = deal(w_s, U8, U8, "w_ds")
+        w_ds_first = keep.tile([P, P], U8, name="w_ds_first", align_bytes=64)
+        w_ds_rest = keep.tile([P, R - P], U8, name="w_ds_rest", align_bytes=64)
+        w_s_dealt = w_s[:].rearrange("p (m t) -> p m t", t=PACK)
+        nc.vector.tensor_copy(w_ds_first[:], w_s_dealt[:, :, 0])
+        nc.vector.tensor_copy(w_ds_rest[:].rearrange("p (t m) -> p m t", t=PACK - 1), w_s_dealt[:, :, 1:PACK])
+        w_ds = [w_ds_first[:]] + [w_ds_rest[:, t * P:(t + 1) * P] for t in range(PACK - 1)]
+        w2_dw = deal(nc.scalar.copy, w2_w, U16, "w2_dw")
         xo_gw = gather_bytes(xo_w, l_xo, U32, "xo_gw")
-        w2_dw = deal(w2_w, U16, U16, "w2_dw")
         xo_gs = gather_bytes(xo_s, l_xo, U8, "xo_gs")
-        w2_ds = deal(w2_s, U8, U8, "w2_ds")
+        w2_ds = deal(nc.vector.tensor_copy, w2_s, U8, "w2_ds")
 
-        stationary = [(w_dw, w_ds, E4M3X4), (w2_dw, w2_ds, E2M1X4)]
+        stationary = [(w_dw, w_ds, E4M3X4), (w2_dw, [w2_ds[:, t * P:(t + 1) * P] for t in range(PACK)], E2M1X4)]
         moving = [(xt_gw, xt_gs, E2M1X4), (xo_gw, xo_gs, E4M3X4)]
 
         def move(on_scalar, dst, src):
@@ -113,54 +119,78 @@ def tile_list_twotab_twoboards_one_tabled_kernel(
         got_a = keep.tile([P, PACK, O], F32, name="got_a")
         got_b = [keep.tile([P, PACK, OH], F32, name=f"got_b{h}") for h in range(HALVES)]
 
+        accs, staged = {}, {}
         for b in range(2):
             sw, ss, sfmt = stationary[b]
             mw, ms, mfmt = moving[b]
-            staged = []
             for t in range(PACK):
                 cols = slice(t * P, (t + 1) * P)
-                acc = psum.tile([P, J], F32, name="acc")
+                accs[b, t] = psum.tile([P, J], F32, name="acc")
                 nc.tensor.matmul_mx(
-                    out=acc[:], lhsT=sw[:, cols].bitcast(sfmt), lhsT_scale=ss[:, cols],
+                    out=accs[b, t][:], lhsT=sw[:, cols].bitcast(sfmt), lhsT_scale=ss[t],
                     rhs=mw[:].bitcast(mfmt), rhs_scale=ms[:], start=True, stop=True,
                 )
                 if (b, t) == (1, 2):
-                    wide = keep.tile([P, N // P, J], F32, name="stage_last", tag="late")
-                    stage = wide[:, 0, :]
+                    staged[b, t] = keep.tile([P, N // P, J], F32, name="stage_last", tag="late")[:, 0, :]
                 else:
-                    stage = keep.tile([P, J], F32, name=f"stage{b}_{t}")[:]
-                staged.append((acc, stage))
-            for pair in range(2):
-                for t in (2 * pair, 2 * pair + 1):
-                    nc.scalar.copy(staged[t][1], staged[t][0][:])
-                for t in (2 * pair, 2 * pair + 1):
-                    move(t % 2 == 0, boards[b][t][:].indirect(l_put[b][:]), staged[t][1])
-            if b == 0:
-                for t in range(PACK):
-                    move(t == 0, got_a[:, t, :], boards[0][t][:].indirect(l_get[0][:]))
+                    staged[b, t] = keep.tile([P, J], F32, name=f"stage{b}_{t}")[:]
+
+        def evacuate(on_scalar, b, t):
+            if on_scalar:
+                nc.scalar.copy(staged[b, t], accs[b, t][:])
+            else:
+                nc.vector.tensor_copy(staged[b, t], accs[b, t][:])
+
+        def put(on_scalar, b, t):
+            move(on_scalar, boards[b][t][:].indirect(l_put[b][:]), staged[b, t])
+
+        def get_a(on_scalar, t):
+            move(on_scalar, got_a[:, t, :], boards[0][t][:].indirect(l_get[0][:]))
 
         cols_h = OH // 16
-        for h in range(HALVES):
-            for t in range(PACK):
-                move(t % 2 == 0, got_b[h][:, t, :], boards[1][t][:].indirect(l_get[1][:, h * cols_h:(h + 1) * cols_h]))
 
-        tz_g = keep.tile([P, N // P, O], F32, name="tz_g", tag="late")
-        for nt in range(N // P):
-            move(True, tz_g[:, nt, :], tz_sb[nt][:].indirect(l_tz[:]))
+        def get_b(on_scalar, h, t):
+            move(on_scalar, got_b[h][:, t, :], boards[1][t][:].indirect(l_get[1][:, h * cols_h:(h + 1) * cols_h]))
 
-        hid, codes, plane = [], [], []
+        evacuate(False, 0, 0)
+        evacuate(True, 0, 1)
+        put(False, 0, 0)
+        put(True, 0, 1)
+        evacuate(True, 0, 2)
+        evacuate(True, 0, 3)
+        put(True, 0, 2)
+        put(True, 0, 3)
+        evacuate(False, 1, 0)
+        put(False, 1, 0)
+        for t in range(1, PACK):
+            evacuate(True, 1, t)
+        put(True, 1, 2)
+        for t in range(PACK):
+            get_a(t == PACK - 1, t)
+        put(False, 1, 1)
+        put(False, 1, 3)
+        for t in (0, 2, 1, 3):
+            get_b(t != PACK - 1, 0, t)
+        for t in (0, 2, 1, 3):
+            get_b(True, 1, t)
+
+        tz_g = keep.tile([P, HALVES, N // P, OH], F32, name="tz_g", tag="late")
         for h in range(HALVES):
-            hid.append(keep.tile([P, OH, PACK], BF16, name=f"hid{h}", align_bytes=64))
+            for nt in range(N // P):
+                move(True, tz_g[:, h, nt, :], tz_sb[nt][:].indirect(l_tz[:, h * cols_h:(h + 1) * cols_h]))
+
+        codes, plane = [], []
+        for h in range(HALVES):
+            hid = keep.tile([P, OH, PACK], BF16, name="hid", align_bytes=64)
             nc.vector.tensor_tensor(
-                hid[h][:].rearrange("p (c i) t -> p c t i", i=4),
+                hid[:].rearrange("p (c i) t -> p c t i", i=4),
                 got_a[:, :, h * OH:(h + 1) * OH].rearrange("p t (c i) -> p c t i", i=4),
                 got_b[h][:].rearrange("p t (c i) -> p c t i", i=4),
                 MAX,
             )
-        for h in range(HALVES):
             codes.append(keep.tile([P, OH], U32, name=f"codes{h}", align_bytes=64))
             plane.append(keep.tile([P, OH], U8, name=f"plane{h}", align_bytes=64))
-            nc.vector.quantize_mx(codes[h][:].bitcast(E5M2X4), plane[h][:], hid[h][:].rearrange("p o t -> p (o t)"))
+            nc.vector.quantize_mx(codes[h][:].bitcast(E5M2X4), plane[h][:], hid[:].rearrange("p o t -> p (o t)"))
         out_v = out.rearrange("(nt p) o -> p nt o", p=P)
         for h in range(HALVES):
             acc = psum.tile([P, N // P, OH], F32, name="acc")
@@ -171,5 +201,5 @@ def tile_list_twotab_twoboards_one_tabled_kernel(
                     rhs=codes[h][:].bitcast(E5M2X4), rhs_scale=plane[h][:], start=True, stop=True,
                 )
             res = keep.tile([P, N // P, OH], F32, name=f"res{h}")
-            nc.vector.tensor_tensor(res[:], acc[:], tz_g[:, :, h * OH:(h + 1) * OH], ADD)
+            nc.vector.tensor_tensor(res[:], acc[:], tz_g[:, h], ADD)
             nc.sync.dma_start(out_v[:, :, h * OH:(h + 1) * OH], res[:])

@@ -56,12 +56,12 @@ def tile_list_twotab_twoboards_one_tabled_kernel(
         xt_s = load_scales(nc.sync, xt_scales, T, "xt_s")
         xt_w = load_words(nc.sync, xt_words[0], U16, T, "xt_w")
         w_w = load_words(nc.sync, w_words[0].rearrange("p n t -> p (n t)"), U32, R, "w_w")
-        w2_w = load_words(nc.gpsimd, w2_words[0], U16, R, "w2_w")
-        l_xo = load_list(offs2, "l_xo")
+        w2_w = load_words(nc.sync, w2_words[0], U16, R, "w2_w")
         w_s = load_scales(nc.sync, w_scales, R, "w_s")
-        xo_w = load_words(nc.sync, xo_words[0].rearrange("p n t -> p (n t)"), U32, Z, "xo_w")
         l_put = [load_list(offs3, "l_put_a")]
+        l_xo = load_list(offs2, "l_xo")
         xo_s = load_scales(nc.sync, xo_scales, Z, "xo_s")
+        xo_w = load_words(nc.sync, xo_words[0].rearrange("p n t -> p (n t)"), U32, Z, "xo_w")
         w2_s = load_scales(nc.sync, w2_scales, R, "w2_s")
         l_get = [load_list(offs5, "l_get_a")]
         l_put.append(load_list(offs4, "l_put_b"))
@@ -78,7 +78,7 @@ def tile_list_twotab_twoboards_one_tabled_kernel(
         boards = [[keep.tile([P, C], F32, name=f"board{b}_{t}") for t in range(PACK)] for b in range(2)]
         for b in range(2):
             for t in range(PACK):
-                nc.gpsimd.memset(boards[b][t][:], 0.0)
+                (nc.vector, nc.gpsimd)[b].memset(boards[b][t][:], 0.0)
 
         def gather_bytes(window, lst, dtype, name):
             tile = keep.tile([P, J], dtype, name=name, align_bytes=64)
@@ -103,8 +103,8 @@ def tile_list_twotab_twoboards_one_tabled_kernel(
         nc.vector.tensor_copy(w_ds_rest[:].rearrange("p (t m) -> p m t", t=PACK - 1), w_s_dealt[:, :, 1:PACK])
         w_ds = [w_ds_first[:]] + [w_ds_rest[:, t * P:(t + 1) * P] for t in range(PACK - 1)]
         w2_dw = deal(nc.scalar.copy, w2_w, U16, "w2_dw")
-        xo_gw = gather_bytes(xo_w, l_xo, U32, "xo_gw")
         xo_gs = gather_bytes(xo_s, l_xo, U8, "xo_gs")
+        xo_gw = gather_bytes(xo_w, l_xo, U32, "xo_gw")
         w2_ds = deal(nc.vector.tensor_copy, w2_s, U8, "w2_ds")
 
         stationary = [(w_dw, w_ds, E4M3X4), (w2_dw, [w2_ds[:, t * P:(t + 1) * P] for t in range(PACK)], E2M1X4)]

@@ -78,7 +78,7 @@ def tile_list_twotab_twoboards_one_tabled_kernel(
         boards = [[keep.tile([P, C], F32, name=f"board{b}_{t}") for t in range(PACK)] for b in range(2)]
         for b in range(2):
             for t in range(PACK):
-                (nc.vector, nc.gpsimd)[b].memset(boards[b][t][:], 0.0)
+                nc.vector.memset(boards[b][t][:].bitcast(I32), 0)
 
         def gather_bytes(window, lst, dtype, name):
             tile = keep.tile([P, J], dtype, name=name, align_bytes=64)
@@ -117,7 +117,7 @@ def tile_list_twotab_twoboards_one_tabled_kernel(
                 nc.vector.tensor_copy(dst, src)
 
         got_a = keep.tile([P, PACK, O], F32, name="got_a")
-        got_b = [keep.tile([P, PACK, OH], F32, name=f"got_b{h}") for h in range(HALVES)]
+        got_b = keep.tile([P, PACK, O], F32, name="got_b")
 
         accs, staged = {}, {}
         for b in range(2):
@@ -130,7 +130,7 @@ def tile_list_twotab_twoboards_one_tabled_kernel(
                     out=accs[b, t][:], lhsT=sw[:, cols].bitcast(sfmt), lhsT_scale=ss[t],
                     rhs=mw[:].bitcast(mfmt), rhs_scale=ms[:], start=True, stop=True,
                 )
-                if (b, t) == (1, 2):
+                if (b, t) == (1, 3):
                     staged[b, t] = keep.tile([P, N // P, J], F32, name="stage_last", tag="late")[:, 0, :]
                 else:
                     staged[b, t] = keep.tile([P, J], F32, name=f"stage{b}_{t}")[:]
@@ -147,10 +147,9 @@ def tile_list_twotab_twoboards_one_tabled_kernel(
         def get_a(on_scalar, t):
             move(on_scalar, got_a[:, t, :], boards[0][t][:].indirect(l_get[0][:]))
 
-        cols_h = OH // 16
-
-        def get_b(on_scalar, h, t):
-            move(on_scalar, got_b[h][:, t, :], boards[1][t][:].indirect(l_get[1][:, h * cols_h:(h + 1) * cols_h]))
+        def get_b(on_scalar, t, first, count):
+            entries = l_get[1][:, first // 16:(first + count) // 16]
+            move(on_scalar, got_b[:, t, first:first + count], boards[1][t][:].indirect(entries))
 
         evacuate(False, 0, 0)
         evacuate(True, 0, 1)
@@ -169,37 +168,32 @@ def tile_list_twotab_twoboards_one_tabled_kernel(
             get_a(t == PACK - 1, t)
         put(False, 1, 1)
         put(False, 1, 3)
-        for t in (0, 2, 1, 3):
-            get_b(t != PACK - 1, 0, t)
-        for t in (0, 2, 1, 3):
-            get_b(True, 1, t)
+        for t in (0, 2, 1):
+            get_b(True, t, 0, O)
+        get_b(False, 3, 0, OH)
+        get_b(True, 3, OH, OH)
 
-        tz_g = keep.tile([P, HALVES, N // P, OH], F32, name="tz_g", tag="late")
-        for h in range(HALVES):
-            for nt in range(N // P):
-                move(True, tz_g[:, h, nt, :], tz_sb[nt][:].indirect(l_tz[:, h * cols_h:(h + 1) * cols_h]))
+        tz_g = keep.tile([P, N // P, O], F32, name="tz_g", tag="late")
+        for nt in range(N // P):
+            move(True, tz_g[:, nt, :], tz_sb[nt][:].indirect(l_tz[:]))
 
-        codes, plane = [], []
-        for h in range(HALVES):
-            hid = keep.tile([P, OH, PACK], BF16, name="hid", align_bytes=64)
-            nc.vector.tensor_tensor(
-                hid[:].rearrange("p (c i) t -> p c t i", i=4),
-                got_a[:, :, h * OH:(h + 1) * OH].rearrange("p t (c i) -> p c t i", i=4),
-                got_b[h][:].rearrange("p t (c i) -> p c t i", i=4),
-                MAX,
+        hid = keep.tile([P, O, PACK], BF16, name="hid", align_bytes=64)
+        nc.vector.tensor_tensor(
+            hid[:].rearrange("p (c i) t -> p c t i", i=4),
+            got_a[:].rearrange("p t (c i) -> p c t i", i=4),
+            got_b[:].rearrange("p t (c i) -> p c t i", i=4),
+            MAX,
+        )
+        codes = keep.tile([P, O], U32, name="codes", align_bytes=64)
+        plane = keep.tile([P, O], U8, name="plane", align_bytes=64)
+        nc.vector.quantize_mx(codes[:].bitcast(E5M2X4), plane[:], hid[:].rearrange("p o t -> p (o t)"))
+        for nt in range(N // P):
+            cols = slice(nt * P, (nt + 1) * P)
+            acc = psum.tile([P, O], F32, name="acc")
+            nc.tensor.matmul_mx(
+                out=acc[:], lhsT=wb_w[:, cols].bitcast(E2M1X4), lhsT_scale=wb_s[:, cols],
+                rhs=codes[:].bitcast(E5M2X4), rhs_scale=plane[:], start=True, stop=True,
             )
-            codes.append(keep.tile([P, OH], U32, name=f"codes{h}", align_bytes=64))
-            plane.append(keep.tile([P, OH], U8, name=f"plane{h}", align_bytes=64))
-            nc.vector.quantize_mx(codes[h][:].bitcast(E5M2X4), plane[h][:], hid[:].rearrange("p o t -> p (o t)"))
-        out_v = out.rearrange("(nt p) o -> p nt o", p=P)
-        for h in range(HALVES):
-            acc = psum.tile([P, N // P, OH], F32, name="acc")
-            for nt in range(N // P):
-                cols = slice(nt * P, (nt + 1) * P)
-                nc.tensor.matmul_mx(
-                    out=acc[:, nt, :], lhsT=wb_w[:, cols].bitcast(E2M1X4), lhsT_scale=wb_s[:, cols],
-                    rhs=codes[h][:].bitcast(E5M2X4), rhs_scale=plane[h][:], start=True, stop=True,
-                )
-            res = keep.tile([P, N // P, OH], F32, name=f"res{h}")
-            nc.vector.tensor_tensor(res[:], acc[:], tz_g[:, h], ADD)
-            nc.sync.dma_start(out_v[:, :, h * OH:(h + 1) * OH], res[:])
+            res = keep.tile([P, O], F32, name=f"res{nt}")
+            nc.vector.tensor_tensor(res[:], acc[:], tz_g[:, nt, :], ADD)
+            nc.sync.dma_start(out[cols, :], res[:])

@@ -38,31 +38,37 @@ def tile_list_twotab_twoboards_one_tabled_kernel(
             return tile
 
         def load_words(queue, src, dtype, cols, name):
-            tile = keep.tile([P, cols], dtype, name=name, align_bytes=64)
+            tile = keep.tile([P, cols], dtype, name=name, tag=name, align_bytes=64)
             queue.dma_start(tile[:].bitcast(I32), src.bitcast(I32))
             return tile
 
-        def load_scales(queue, src, cols, name):
-            tile = keep.tile([P, cols], U8, name=name, align_bytes=64)
-            rows = src[0].bitcast(I32)
-            for q in range(4):
-                queue.dma_start(
-                    tile[32 * q:32 * (q + 1), :].bitcast(I32),
-                    rows[4 * q:4 * (q + 1), :].unsqueeze(0).to_broadcast([8, 4, cols // 4]),
-                )
+        def cleared_plane(cols, name):
+            tile = keep.tile([P, cols], U8, name=name, tag=name, align_bytes=64)
+            nc.vector.memset(tile[:].bitcast(I32), 0)
             return tile
 
+        def load_scales(tile, src):
+            rows = src[0].bitcast(I32)
+            for q in range(4):
+                nc.sync.dma_start(tile[32 * q:32 * q + 4, :].bitcast(I32), rows[4 * q:4 * (q + 1), :])
+
+        xt_s = cleared_plane(T, "xt_s")
+        w_s = cleared_plane(R, "w_s")
+        xo_s = cleared_plane(Z, "xo_s")
+        w2_s = cleared_plane(R, "w2_s")
+        wb_s = cleared_plane(N, "wb_s")
+
         l_xt = load_list(offs, "l_xt")
-        xt_s = load_scales(nc.sync, xt_scales, T, "xt_s")
+        l_put = [load_list(offs3, "l_put_a")]
+        load_scales(xt_s, xt_scales)
         xt_w = load_words(nc.sync, xt_words[0], U16, T, "xt_w")
         w_w = load_words(nc.sync, w_words[0].rearrange("p n t -> p (n t)"), U32, R, "w_w")
+        load_scales(w_s, w_scales)
         w2_w = load_words(nc.sync, w2_words[0], U16, R, "w2_w")
-        w_s = load_scales(nc.sync, w_scales, R, "w_s")
-        l_put = [load_list(offs3, "l_put_a")]
         l_xo = load_list(offs2, "l_xo")
-        xo_s = load_scales(nc.sync, xo_scales, Z, "xo_s")
+        load_scales(xo_s, xo_scales)
         xo_w = load_words(nc.sync, xo_words[0].rearrange("p n t -> p (n t)"), U32, Z, "xo_w")
-        w2_s = load_scales(nc.sync, w2_scales, R, "w2_s")
+        load_scales(w2_s, w2_scales)
         l_get = [load_list(offs5, "l_get_a")]
         l_put.append(load_list(offs4, "l_put_b"))
         l_get.append(load_list(offs6, "l_get_b"))
@@ -73,12 +79,15 @@ def tile_list_twotab_twoboards_one_tabled_kernel(
             nc.sync.dma_start(tile[:], tz[nt * P:(nt + 1) * P, :])
             tz_sb.append(tile)
         wb_w = load_words(nc.sync, wb_words[0], U16, N, "wb_w")
-        wb_s = load_scales(nc.sync, wb_scales, N, "wb_s")
+        load_scales(wb_s, wb_scales)
 
-        boards = [[keep.tile([P, C], F32, name=f"board{b}_{t}") for t in range(PACK)] for b in range(2)]
-        for b in range(2):
-            for t in range(PACK):
-                nc.vector.memset(boards[b][t][:].bitcast(I32), 0)
+        reused = {(1, 2): "w_w", (1, 3): "w_s"}
+        boards = [
+            [keep.tile([P, C], F32, name=f"board{b}_{t}", tag=reused.get((b, t), f"board{b}_{t}"), align_bytes=64) for t in range(PACK)]
+            for b in range(2)
+        ]
+        for t in range(PACK):
+            nc.vector.memset(boards[0][t][:].bitcast(I32), 0)
 
         def gather_bytes(window, lst, dtype, name):
             tile = keep.tile([P, J], dtype, name=name, align_bytes=64)
@@ -102,6 +111,8 @@ def tile_list_twotab_twoboards_one_tabled_kernel(
         nc.vector.tensor_copy(w_ds_first[:], w_s_dealt[:, :, 0])
         nc.vector.tensor_copy(w_ds_rest[:].rearrange("p (t m) -> p m t", t=PACK - 1), w_s_dealt[:, :, 1:PACK])
         w_ds = [w_ds_first[:]] + [w_ds_rest[:, t * P:(t + 1) * P] for t in range(PACK - 1)]
+        for t in range(PACK):
+            nc.vector.memset(boards[1][t][:].bitcast(I32), 0)
         w2_dw = deal(nc.scalar.copy, w2_w, U16, "w2_dw")
         xo_gs = gather_bytes(xo_s, l_xo, U8, "xo_gs")
         xo_gw = gather_bytes(xo_w, l_xo, U32, "xo_gw")

from contextlib import ExitStack

import concourse.mybir as mybir

F32 = mybir.dt.float32
BF16 = mybir.dt.bfloat16
I32 = mybir.dt.int32
U32 = mybir.dt.uint32
U16 = mybir.dt.uint16
U8 = mybir.dt.uint8
E4M3X4 = mybir.dt.float8_e4m3fn_x4
E5M2X4 = mybir.dt.float8_e5m2_x4
E2M1X4 = mybir.dt.float4_e2m1fn_x4
COPY = mybir.ActivationFunctionType.Copy
MAX = mybir.AluOpType.max
ADD = mybir.AluOpType.add

P = 128
PACK = 4
T, Z, J, R, C, O, N, E = 1024, 1024, 256, 512, 512, 256, 256, 1024
HALVES = 2
OH = O // HALVES
FLOPS = 2 * 512 * R * J * 2 + 2 * R * N * O


def tile_list_twotab_twoboards_one_tabled_kernel(
    tc, xt_words, xt_scales, w_words, w_scales, xo_words, xo_scales, w2_words, w2_scales,
    wb_words, wb_scales, tz, offs, offs2, offs3, offs4, offs5, offs6, offs7, out,
):
    nc = tc.nc
    with ExitStack() as ctx:
        keep = ctx.enter_context(tc.tile_pool(name="keep", bufs=1))
        psum = ctx.enter_context(tc.psum_pool(name="psum", bufs=8))

        def load_list(src, name):
            tile = keep.tile([P, src.shape[1]], U16, name=name)
            nc.sync.dma_start(tile[:], src)
            return tile

        def load_words(queue, src, dtype, cols, name):
            tile = keep.tile([P, cols], dtype, name=name, tag=name, align_bytes=64)
            queue.dma_start(tile[:].bitcast(I32), src.bitcast(I32))
            return tile

        def cleared_plane(cols, name):
            tile = keep.tile([P, cols], U8, name=name, tag=name, align_bytes=64)
            nc.vector.memset(tile[:].bitcast(I32), 0)
            return tile

        def load_scales(tile, src):
            rows = src[0].bitcast(I32)
            for q in range(4):
                nc.sync.dma_start(tile[32 * q:32 * q + 4, :].bitcast(I32), rows[4 * q:4 * (q + 1), :])

        xt_s = cleared_plane(T, "xt_s")
        w_s = cleared_plane(R, "w_s")
        xo_s = cleared_plane(Z, "xo_s")
        w2_s = cleared_plane(R, "w2_s")
        wb_s = cleared_plane(N, "wb_s")

        l_xt = load_list(offs, "l_xt")
        l_put = [load_list(offs3, "l_put_a")]
        load_scales(xt_s, xt_scales)
        xt_w = load_words(nc.sync, xt_words[0], U16, T, "xt_w")
        w_w = load_words(nc.sync, w_words[0].rearrange("p n t -> p (n t)"), U32, R, "w_w")
        load_scales(w_s, w_scales)
        w2_w = load_words(nc.sync, w2_words[0], U16, R, "w2_w")
        l_xo = load_list(offs2, "l_xo")
        load_scales(xo_s, xo_scales)
        xo_w = load_words(nc.sync, xo_words[0].rearrange("p n t -> p (n t)"), U32, Z, "xo_w")
        load_scales(w2_s, w2_scales)
        l_get = [load_list(offs5, "l_get_a")]
        l_put.append(load_list(offs4, "l_put_b"))
        l_get.append(load_list(offs6, "l_get_b"))
        l_tz = load_list(offs7, "l_tz")
        tz_sb = []
        for nt in range(N // P):
            tile = keep.tile([P, E], F32, name=f"tz{nt}")
            nc.sync.dma_start(tile[:], tz[nt * P:(nt + 1) * P, :])
            tz_sb.append(tile)
        wb_w = load_words(nc.sync, wb_words[0], U16, N, "wb_w")
        load_scales(wb_s, wb_scales)

        reused = {(1, 2): "w_w", (1, 3): "w_s"}
        boards = [
            [keep.tile([P, C], F32, name=f"board{b}_{t}", tag=reused.get((b, t), f"board{b}_{t}"), align_bytes=64) for t in range(PACK)]
            for b in range(2)
        ]
        for t in range(PACK):
            nc.vector.memset(boards[0][t][:].bitcast(I32), 0)

        def gather_bytes(window, lst, dtype, name):
            tile = keep.tile([P, J], dtype, name=name, align_bytes=64)
            nc.vector.tensor_copy(tile[:], window[:].indirect(lst[:]))
            return tile

        def deal(copy, src, dtype, name):
            tile = keep.tile([P, R], dtype, name=name, align_bytes=64)
            copy(
                tile[:].rearrange("p (t m) -> p m t", t=PACK),
                src[:].rearrange("p (m t) -> p m t", t=PACK),
            )
            return tile

        xt_gw = gather_bytes(xt_w, l_xt, U16, "xt_gw")
        w_dw = deal(nc.scalar.copy, w_w, U32, "w_dw")
        xt_gs = gather_bytes(xt_s, l_xt, U8, "xt_gs")
        w_ds_first = keep.tile([P, P], U8, name="w_ds_first", align_bytes=64)
        w_ds_rest = keep.tile([P, R - P], U8, name="w_ds_rest", align_bytes=64)
        w_s_dealt = w_s[:].rearrange("p (m t) -> p m t", t=PACK)
        nc.vector.tensor_copy(w_ds_first[:], w_s_dealt[:, :, 0])
        nc.vector.tensor_copy(w_ds_rest[:].rearrange("p (t m) -> p m t", t=PACK - 1), w_s_dealt[:, :, 1:PACK])
        w_ds = [w_ds_first[:]] + [w_ds_rest[:, t * P:(t + 1) * P] for t in range(PACK - 1)]
        for t in range(PACK):
            nc.vector.memset(boards[1][t][:].bitcast(I32), 0)
        w2_dw = deal(nc.scalar.copy, w2_w, U16, "w2_dw")
        xo_gs = gather_bytes(xo_s, l_xo, U8, "xo_gs")
        xo_gw = gather_bytes(xo_w, l_xo, U32, "xo_gw")
        w2_ds = deal(nc.vector.tensor_copy, w2_s, U8, "w2_ds")

        stationary = [(w_dw, w_ds, E4M3X4), (w2_dw, [w2_ds[:, t * P:(t + 1) * P] for t in range(PACK)], E2M1X4)]
        moving = [(xt_gw, xt_gs, E2M1X4), (xo_gw, xo_gs, E4M3X4)]

        def move(on_scalar, dst, src):
            if on_scalar:
                nc.scalar.activation(dst, src, COPY)
            else:
                nc.vector.tensor_copy(dst, src)

        got_a = keep.tile([P, PACK, O], F32, name="got_a")
        got_b = keep.tile([P, PACK, O], F32, name="got_b")

        accs, staged = {}, {}
        for b in range(2):
            sw, ss, sfmt = stationary[b]
            mw, ms, mfmt = moving[b]
            for t in range(PACK):
                cols = slice(t * P, (t + 1) * P)
                accs[b, t] = psum.tile([P, J], F32, name="acc")
                nc.tensor.matmul_mx(
                    out=accs[b, t][:], lhsT=sw[:, cols].bitcast(sfmt), lhsT_scale=ss[t],
                    rhs=mw[:].bitcast(mfmt), rhs_scale=ms[:], start=True, stop=True,
                )
                if (b, t) == (1, 3):
                    staged[b, t] = keep.tile([P, N // P, J], F32, name="stage_last", tag="late")[:, 0, :]
                else:
                    staged[b, t] = keep.tile([P, J], F32, name=f"stage{b}_{t}")[:]

        def evacuate(on_scalar, b, t):
            if on_scalar:
                nc.scalar.copy(staged[b, t], accs[b, t][:])
            else:
                nc.vector.tensor_copy(staged[b, t], accs[b, t][:])

        def put(on_scalar, b, t):
            move(on_scalar, boards[b][t][:].indirect(l_put[b][:]), staged[b, t])

        def get_a(on_scalar, t):
            move(on_scalar, got_a[:, t, :], boards[0][t][:].indirect(l_get[0][:]))

        def get_b(on_scalar, t, first, count):
            entries = l_get[1][:, first // 16:(first + count) // 16]
            move(on_scalar, got_b[:, t, first:first + count], boards[1][t][:].indirect(entries))

        evacuate(False, 0, 0)
        evacuate(True, 0, 1)
        put(False, 0, 0)
        put(True, 0, 1)
        evacuate(True, 0, 2)
        evacuate(True, 0, 3)
        put(True, 0, 2)
        put(True, 0, 3)
        evacuate(False, 1, 0)
        put(False, 1, 0)
        for t in range(1, PACK):
            evacuate(True, 1, t)
        put(True, 1, 2)
        for t in range(PACK):
            get_a(t == PACK - 1, t)
        put(False, 1, 1)
        put(False, 1, 3)
        for t in (0, 2, 1):
            get_b(True, t, 0, O)
        get_b(False, 3, 0, OH)
        get_b(True, 3, OH, OH)

        tz_g = keep.tile([P, N // P, O], F32, name="tz_g", tag="late")
        for nt in range(N // P):
            move(True, tz_g[:, nt, :], tz_sb[nt][:].indirect(l_tz[:]))

        hid = keep.tile([P, O, PACK], BF16, name="hid", align_bytes=64)
        nc.vector.tensor_tensor(
            hid[:].rearrange("p (c i) t -> p c t i", i=4),
            got_a[:].rearrange("p t (c i) -> p c t i", i=4),
            got_b[:].rearrange("p t (c i) -> p c t i", i=4),
            MAX,
        )
        codes = keep.tile([P, O], U32, name="codes", align_bytes=64)
        plane = keep.tile([P, O], U8, name="plane", align_bytes=64)
        nc.vector.quantize_mx(codes[:].bitcast(E5M2X4), plane[:], hid[:].rearrange("p o t -> p (o t)"))
        for nt in range(N // P):
            cols = slice(nt * P, (nt + 1) * P)
            acc = psum.tile([P, O], F32, name="acc")
            nc.tensor.matmul_mx(
                out=acc[:], lhsT=wb_w[:, cols].bitcast(E2M1X4), lhsT_scale=wb_s[:, cols],
                rhs=codes[:].bitcast(E5M2X4), rhs_scale=plane[:], start=True, stop=True,
            )
            res = keep.tile([P, O], F32, name=f"res{nt}")
            nc.vector.tensor_tensor(res[:], acc[:], tz_g[:, nt, :], ADD)
            nc.sync.dma_start(out[cols, :], res[:])
